import numpy as np
CORES = [21,109,149,237,277,365,405,493,150,406]
N = 10
F = 64
def setup_inputs(rng):
    return {"a": rng.standard_normal((N, 128, 128), dtype=np.float32), "w": rng.standard_normal((N, 128, F), dtype=np.float32)}
def setup_inputs_big(rng):
    d = setup_inputs(rng)
    for k in ("a", "w"): d[k] = (d[k].astype(np.float32) * 1024.0).astype(d[k].dtype)
    return d
def setup_inputs_small(rng):
    d = setup_inputs(rng)
    for k in ("a", "w"): d[k] = (d[k].astype(np.float32) * (1 / 1024.0)).astype(d[k].dtype)
    return d
def setup_inputs_apart(rng):
    d = setup_inputs(rng)
    f = (10.0 ** rng.permutation(np.linspace(-1.5, 1.5, N))).astype(np.float32).reshape(N, 1, 1)
    for k in ("a", "w"): d[k] = (d[k].astype(np.float32) * f).astype(d[k].dtype)
    return d
def reference(a, w):
    A, W = a.astype(np.float64), w.astype(np.float64)
    p = np.stack([A[j].T @ W[j] for j in range(N)])
    return {"y": np.cumsum(p, axis=0).astype(np.float32 if a.dtype != np.float64 else np.float64)}

from concourse.bass import DstId, RemoteDMATransfer
from concourse.mybir import AluOpType

N = 10
F = 64
WIDTH = 8


def _rank(i):
    return ("rank", i, 0)


def _aide(i, n=0):
    return ("aide", i, n)


FOLDS = [
    (_aide(1, 0), (1, 7), (9, 8)),
    (_aide(1, 1), (1,), (2, 6)),
    (_aide(3), (1, 3), (4,)),
    (_aide(5), (3, 5), (8, 6, 9)),
    (_aide(0), (0,), (1,)),
    (_aide(4), (2,), (7,)),
    (_rank(9), (0, 4, 6), (7,)),
    (_rank(8), (0, 2), (3,)),
    (_rank(8), (0, 2, 4), (5,)),
    (_rank(4), (2, 4), (6,)),
    (_rank(4), (2, 8), (9,)),
    (_rank(0), (6,), (8,)),
    (_rank(2), (0,), (4,)),
    (_rank(3), (1,), (5,)),
    (_rank(5), (3, 5), (7,)),
]


def _schedule():
    raw = [[] for _ in range(N)]
    load = {}
    for node, srcs, dsts in FOLDS:
        load[node] = load.get(node, 0) + len(dsts)
        for s in srcs:
            if node != _rank(s) and node not in raw[s]:
                raw[s].append(node)
    for r in range(N):
        have = [s for _, srcs, dsts in FOLDS if r in dsts for s in srcs]
        have += [j for j in range(r) if _rank(r) in raw[j]]
        assert len(have) == len(set(have)) and all(j < r for j in have)
        for j in range(r):
            if j not in have:
                raw[j].append(_rank(r))

    def late(node):
        return node[0] == "aide" or not raw[node[1]]

    def urgency(node):
        if node not in load:
            return (2, 0)
        return (0 if late(node) else 1, -load[node])

    msgs = []
    for j in range(N):
        raw[j].sort(key=urgency)
        if raw[j]:
            msgs.append((_rank(j), (j,), tuple(raw[j]), 0, 1))
    for node, srcs, dsts in FOLDS:
        n = len([1 for other, _, _ in FOLDS if other == node])
        msgs.append((node, srcs, tuple(_rank(d) for d in dsts), 1, n))
    slot, eta = {}, {}
    for m, (node, srcs, dsts, call, n) in enumerate(msgs):
        if call == 0:
            start = 0
        else:
            feeds = [eta[(s, node)] for s in srcs if node != _rank(s)]
            start = max(feeds) + 4 + (5 if late(node) else 0)
        for i, d in enumerate(dsts):
            slot[(m, d)] = len([1 for k in slot if k[1] == d])
            if call == 0:
                eta[(srcs[0], d)] = i + 1
            eta[(m, d, "msg")] = start + (i + 1) * n
    return msgs, slot, eta


MSGS, SLOT, ETA = _schedule()
SLOTS = 1 + max(SLOT.values())

SCRATCH = {
    "a_sb": ("sbuf", [128, 128], "float32"),
    "w_sb": ("sbuf", [128, F], "float32"),
    "ps": ("psum", [128, F], "float32"),
    "p_sb": ("sbuf", [128, F], "float32"),
    "acc": ("sbuf", [128, F], "float32"),
    "land": ("sbuf", [128, SLOTS * F], "float32"),
}
SEMAPHORES = ["ld", "mm", "cp", "vs", "st", "snt"] + ["m%d" % m for m in range(len(MSGS))]

_CACHE = {}


def _take(avail, skip, count):
    out, seen, b = 0, 0, 0
    while count and (avail >> b):
        if (avail >> b) & 1:
            if seen >= skip:
                out |= 1 << b
                count -= 1
            seen += 1
        b += 1
    assert count == 0
    return out


def _wiring(T, topo):
    key = tuple(T.cores)
    if key in _CACHE:
        return _CACHE[key]
    place = {_rank(i): c for i, c in enumerate(T.cores)}
    for node, _, _ in FOLDS:
        if node in place:
            continue
        home = T.cores[node[1]]
        serves = [T.cores[d] for other, _, dsts in FOLDS if other == node for d in dsts]
        for q in range(max(0, home - 16), home + 16):
            if (topo.host(q) == topo.host(home) and topo.chip(q) == topo.chip(home) and topo.die(q) == topo.die(home)
                    and q not in place.values() and all(topo.may_write(q, d) for d in serves)):
                place[node] = q
                break
        assert node in place
    masks = {}
    for node in set(m[0] for m in MSGS):
        for call in (0, 1):
            mine = [m for m, x in enumerate(MSGS) if x[0] == node and x[3] == call]
            if not mine:
                continue
            avail = -1
            for m in mine:
                for d in MSGS[m][2]:
                    assert topo.may_write(place[node], place[d])
                    avail &= topo.mask(place[node], place[d])
            room = min(WIDTH, len([b for b in range(64) if (avail >> b) & 1])) // len(mine)
            per = 1
            while per * 2 <= room:
                per *= 2
            for i, m in enumerate(mine):
                masks[m] = (_take(avail, i * per, per), per)
    _CACHE[key] = (place, masks)
    return _CACHE[key]


def rank_program(g, core, T, topo):
    place, masks = _wiring(T, topo)
    here = [n for n, c in place.items() if c == core]
    if not here:
        return
    node = here[0]
    sem = T.sem
    is_rank = node[0] == "rank"
    rank = node[1] if is_rank else None

    def landing(m, d):
        s = SLOT[(m, d)]
        return T.land[:, s * F:(s + 1) * F]

    raw_from = {x[1][0]: m for m, x in enumerate(MSGS) if x[3] == 0}
    sends_raw = is_rank and rank in raw_from

    if is_rank:
        g.sync.dma_start(out=T.a_sb[:, :], in_=T.a[:, :]).then_inc(sem.ld, 16)
        g.scalar.dma_start(out=T.w_sb[:, :], in_=T.w[:, :]).then_inc(sem.ld, 16)
        g.tensor.wait_ge(sem.ld, 32)
        g.tensor.matmul(T.ps[:, :], T.a_sb[:, :], T.w_sb[:, :], start=True, stop=True).then_inc(sem.mm, 1)
        g.vector.wait_ge(sem.mm, 1)
        if sends_raw:
            g.vector.tensor_copy(out=T.p_sb[:, :], in_=T.ps[:, :]).then_inc(sem.cp, 1)

    sent = 0
    for call in (0, 1):
        mine = [m for m, x in enumerate(MSGS) if x[0] == node and x[3] == call]
        if not mine:
            continue
        if call == 0:
            g.wait_ge(sem.cp, 1)
        else:
            feeds = sorted(set(raw_from[s] for m in mine for s in MSGS[m][1] if _rank(s) != node),
                           key=lambda f: ETA[(f, node, "msg")])
            for f in feeds:
                g.wait_ge(sem["m%d" % f], masks[f][1])
        transfers = []
        for m in mine:
            _, srcs, dsts, _, _ = MSGS[m]
            aps = [T.p_sb[:, :] if _rank(s) == node else landing(raw_from[s], node) for s in srcs]
            ids = []
            for d in dsts:
                rid, pid = topo.addr(place[d], core)
                ids.append(DstId(rid=rid, pnc=pid))
            transfers.append(RemoteDMATransfer(dst_ids=ids, dma_engine_mask=masks[m][0], remote_sem=sem["m%d" % m],
                                               srcs=aps, dsts=[landing(m, d) for d in dsts],
                                               alu_op=1 if len(aps) > 1 else 0))
            sent += masks[m][1]
        g.remote_dma_fused(transfers, local_sem=sem.snt)

    if is_rank:
        terms = [m for m, x in enumerate(MSGS) if node in x[2] and all(s < rank for s in x[1])]
        terms.sort(key=lambda m: ETA[(m, node, "msg")])
        for i, m in enumerate(terms):
            g.vector.wait_ge(sem["m%d" % m], masks[m][1])
            if i:
                g.vector.wait_ge(sem.vs, i)
            first = T.ps[:, :] if i == 0 else T.acc[:, :]
            g.vector.tensor_tensor(out=T.acc[:, :], in0=first, in1=landing(m, node),
                                   op=AluOpType.add).then_inc(sem.vs, 1)
        if terms:
            g.sync.wait_ge(sem.vs, len(terms))
            g.sync.dma_start(out=T.y[:, :], in_=T.acc[:, :]).then_inc(sem.st, 16)
        else:
            g.sync.wait_ge(sem.cp, 1)
            g.sync.dma_start(out=T.y[:, :], in_=T.p_sb[:, :]).then_inc(sem.st, 16)
        g.sync.wait_ge(sem.st, 16)
    if sent:
        g.wait_ge(sem.snt, sent)
